import numpy as np
import ml_dtypes


def mxq(x, axis, fmt="e4m3"):
    dtype, down = {"e4m3": (ml_dtypes.float8_e4m3fn, 7), "e5m2": (ml_dtypes.float8_e5m2, 14)}[fmt]
    v = np.moveaxis(np.asarray(x, np.float32).astype(ml_dtypes.bfloat16).astype(np.float64), axis, -1)
    blocks = v.reshape(v.shape[:-1] + (-1, 32))
    amax = np.abs(blocks).max(-1, keepdims=True)
    byte = np.maximum(np.where(amax > 0, np.frexp(amax)[1] - 1 + 127, 0) - down, 1)
    scale = np.exp2(byte - 127.0)
    codes = (blocks / scale).astype(np.float32).astype(dtype).astype(np.float64)
    return np.moveaxis((codes * scale).reshape(v.shape), -1, axis)


WIDE = False


def mx_kscale(k):
    if not WIDE:
        return np.ones(k)
    levels = np.array([10, -10, 5, -5, 0])
    if k % 512:
        return np.exp2(np.random.permutation(np.resize(levels, k // 32))).repeat(32)
    a = np.empty((k // 512, 16))
    for p in range(k // 512):
        a[p, :8] = np.random.permutation(np.resize(levels, 8))
        for g in range(8):
            far = levels[np.abs(levels - a[p, g]) >= 10]
            a[p, g + 8] = far[np.random.randint(len(far))]
    return np.exp2(a.ravel()).repeat(32)


BF16 = ml_dtypes.bfloat16


def bf(x):
    return np.asarray(x, np.float32).astype(BF16)


def f64(x):
    return np.asarray(x).astype(np.float64)


E2M1 = np.array([0.0, 0.5, 1.0, 1.5, 2.0, 3.0, 4.0, 6.0, -0.0, -0.5, -1.0, -1.5, -2.0, -3.0, -4.0, -6.0])


def pack_weight(w, fmt):
    k, n = w.shape
    w = f64(bf(w)).reshape(k // 32, 32, n)
    amax = np.abs(w).max(1)
    if fmt == "e4m3":
        byte = np.frexp(amax)[1] - 1 + 127 - 7
    else:
        mant, ex = np.frexp(amax / 6.0)
        byte = np.where(mant > 0.5, ex, ex - 1) + 127
    byte = np.clip(np.where(amax > 0, byte, 1), 1, 254)
    scaled = (w * np.exp2(127.0 - byte)[:, None, :]).reshape(k, n).astype(np.float32)
    by_word = np.ascontiguousarray(scaled.reshape(k // 512, 128, 4, n).transpose(0, 1, 3, 2))
    if fmt == "e4m3":
        words = by_word.astype(ml_dtypes.float8_e4m3fn).view(np.uint8)
    else:
        c = by_word.astype(ml_dtypes.float4_e2m1fn).view(np.uint8) & 0xF
        words = c[..., 0::2] | (c[..., 1::2] << 4)
    return np.ascontiguousarray(words), np.ascontiguousarray(byte.astype(np.uint8).reshape(k // 512, 16, n))


def unpack_weight(words, scales, fmt):
    g, p, n, _ = words.shape
    if fmt == "e4m3":
        vals = np.ascontiguousarray(words).view(ml_dtypes.float8_e4m3fn).astype(np.float64)
    else:
        nib = np.empty((g, p, n, 4), np.uint8)
        nib[..., 0::2] = words & 0xF
        nib[..., 1::2] = words >> 4
        vals = E2M1[nib]
    vals = vals * np.repeat(np.exp2(scales.astype(np.float64) - 127.0), 8, axis=1)[..., None]
    return vals.transpose(0, 1, 3, 2).reshape(g * 512, n)
def pack4(w):
    words, scales = pack_weight(w, "e2m1")
    return words.reshape(words.shape[0], 128, -1), scales


def unpack4(words, scales):
    return unpack_weight(words.reshape(words.shape[0], 128, -1, 2), scales, "e2m1")


M, K, Z, D, T = 512, 1024, 4, 1024, 512


def sigmoid(v):
    return 1.0 / (1.0 + np.exp(-v))


def draw0():
    s, t = mx_kscale(K), mx_kscale(D)
    x = np.random.standard_normal((M, K)) * s
    phi = 0.5 * np.random.standard_normal((M, D)) * t
    w_psi = np.random.standard_normal((K, Z * D)) / np.sqrt(K) / s[:, None] * np.tile(t, Z)
    b_psi = 0.3 * np.random.standard_normal((Z, D)) * t
    w_gamma = np.random.standard_normal((K, D)) / np.sqrt(K) / s[:, None]
    b_gamma = 1.0 + 0.3 * np.random.standard_normal(D)
    w_pref = 2.0 * np.random.standard_normal((D, T)) / np.sqrt(D) / t[:, None]
    beta = 2.0 + 0.3 * np.random.standard_normal(T)
    psi_words, psi_scales = pack4(w_psi)
    gamma_words, gamma_scales = pack4(w_gamma)
    pref_words, pref_scales = pack4(w_pref)
    return {"x": bf(x), "phi": bf(phi),
            "psi_words": psi_words, "psi_scales": psi_scales, "b_psi": bf(b_psi),
            "gamma_words": gamma_words, "gamma_scales": gamma_scales, "b_gamma": bf(b_gamma),
            "pref_words": pref_words, "pref_scales": pref_scales, "beta": bf(beta)}


def core(x, phi, psi_words, psi_scales, b_psi, gamma_words, gamma_scales, b_gamma, pref_words, pref_scales, beta):
    xq = mxq(f64(x), 1, "e4m3")
    future = (xq @ unpack4(psi_words, psi_scales)).reshape(M, Z, D) + f64(b_psi)
    future = np.maximum(future, 0.0)
    gamma = sigmoid((xq @ unpack4(gamma_words, gamma_scales)) + f64(b_gamma))
    psi = f64(phi)[:, None, :] + gamma[:, None, :] * future
    val = (mxq(psi.reshape(M * Z, D), 1, "e4m3") @ unpack4(pref_words, pref_scales)).reshape(M, Z, T)
    best = np.max(val, axis=1)
    e = np.exp(f64(beta) * (val - best[:, None, :]))
    soft = np.sum(e * val, axis=1) / np.sum(e, axis=1)
    return best, soft


def e4m3fn_bytes(y):
    return np.clip(np.asarray(y, np.float64), -448.0, 448.0).astype(np.float32).astype(ml_dtypes.float8_e4m3fn).view(np.uint8)


def e4m3fn_values(b):
    return np.asarray(b, np.uint8).view(ml_dtypes.float8_e4m3fn).astype(np.float64)


def setup_inputs():
    d = draw0()
    x0 = np.asarray(d['x']).astype(np.float64)
    s = (np.max(np.abs(x0), axis=(0,), keepdims=True) / 448.0).astype(np.float32)
    out = {}
    for k, v in d.items():
        if k == 'x':
            out['x_bytes'] = e4m3fn_bytes(x0 / s.astype(np.float64))
            out['x_scale'] = s
        else:
            out[k] = v
    return out


def reference(x_bytes, x_scale, phi, psi_words, psi_scales, b_psi, gamma_words, gamma_scales, b_gamma, pref_words, pref_scales, beta):
    return core(e4m3fn_values(x_bytes) * x_scale.astype(np.float64), phi, psi_words, psi_scales, b_psi, gamma_words, gamma_scales, b_gamma, pref_words, pref_scales, beta)

@@ -1,0 +1,329 @@
+from contextlib import ExitStack
+
+import concourse.mybir as mybir
+from concourse.masks import make_identity
+
+F32 = mybir.dt.float32
+BF16 = mybir.dt.bfloat16
+U8 = mybir.dt.uint8
+I32 = mybir.dt.int32
+U32 = mybir.dt.uint32
+FP8 = mybir.dt.float8_e4m3fn
+E4X4 = mybir.dt.float8_e4m3fn_x4
+E2X4 = mybir.dt.float4_e2m1fn_x4
+ACT = mybir.ActivationFunctionType
+ALU = mybir.AluOpType
+
+P = 128
+M, K, Z, D, T = 512, 1024, 4, 1024, 512
+G = 2
+MT = M // P
+DT = D // P
+TT = T // P
+
+FLOPS = 2 * M * K * (Z * D + D) + 2 * M * Z * D * T
+
+
+def tile_successor_feature_gpi_f1_kernel(
+    tc, x_bytes, x_scale, phi, psi_words, psi_scales, b_psi, gamma_words, gamma_scales,
+    b_gamma, pref_words, pref_scales, beta, out_0, out_1,
+):
+    nc = tc.nc
+    with ExitStack() as ctx:
+        keep = ctx.enter_context(tc.tile_pool(name="keep", bufs=1))
+        work = ctx.enter_context(tc.tile_pool(name="work", bufs=2))
+        psum = ctx.enter_context(tc.psum_pool(name="psum", bufs=4))
+        ctx.enter_context(tc.manual_schedule())
+
+        def w4(shape, dtype, name):
+            return work.tile(shape, dtype, name=name, tag="w4", bufs=15, align_bytes=64)
+
+        x_sc = keep.tile([P, G, 4], F32, name="x_sc")
+        nc.scalar.dma_start(out=x_sc[:], in_=x_scale.rearrange("o (g p t) -> p (o g) t", g=G, p=P, t=4))
+        xb = []
+        for mt in range(MT):
+            xb_t = keep.tile([P, K], U8, name="xb%d" % mt)
+            nc.sync.dma_start(out=xb_t[:], in_=x_bytes[mt * P : (mt + 1) * P, :])
+            xb.append(xb_t)
+
+        ident_f = keep.tile([P, P], F32, name="ident_f")
+        make_identity(nc, ident_f[:])
+        ident_b = keep.tile([P, P], BF16, name="ident_b")
+        rows = keep.tile([P, P], BF16, name="rows")
+        gam_sc = keep.tile([P, G, D], U8, name="gam_sc", align_bytes=64)
+        psi_sc = keep.tile([P, G, Z * D], U8, name="psi_sc", align_bytes=64)
+        pref_sc = keep.tile([P, G, T], U8, name="pref_sc", align_bytes=64)
+        nc.vector.memset(gam_sc[:].rearrange("p g n -> p (g n)").bitcast(I32), 0)
+        nc.gpsimd.memset(rows[:], 0.0)
+        nc.gpsimd.memset(psi_sc[:].rearrange("p g n -> p (g n)").bitcast(I32), 0)
+        nc.gpsimd.memset(pref_sc[:].rearrange("p g n -> p (g n)").bitcast(I32), 0)
+        nc.vector.tensor_copy(out=ident_b[:], in_=ident_f[:])
+        warm = keep.tile([P, 1], F32, name="warm")
+        nc.scalar.activation(out=warm[:], in_=ident_f[:, 0:1], func=ACT.Sigmoid)
+
+        def load_scales(plane, dram):
+            for q in range(4):
+                nc.sync.dma_start(
+                    out=plane[32 * q : 32 * q + 4, :, :].bitcast(I32),
+                    in_=dram[:, 4 * q : 4 * q + 4, :].rearrange("g q n -> q g n").bitcast(I32),
+                )
+
+        gam_w = keep.tile([P, G, 2 * D], U8, name="gam_w", align_bytes=64)
+        psi_w = [keep.tile([P, G, 2 * D], U8, name="psi_w%d" % z, align_bytes=64) for z in range(Z)]
+        pref_w = keep.tile([P, G, 2 * T], U8, name="pref_w", align_bytes=64)
+        phi_sb = keep.tile([P, MT, D], BF16, name="phi_sb")
+
+        def load_words(tile, dram):
+            nc.sync.dma_start(out=tile[:].bitcast(I32), in_=dram.rearrange("g p b -> p g b").bitcast(I32))
+
+        load_scales(gam_sc, gamma_scales)
+        load_scales(psi_sc, psi_scales)
+        load_words(gam_w, gamma_words)
+        load_words(psi_w[0], psi_words[:, :, 0 : 2 * D])
+        nc.sync.dma_start(out=rows[0:32, :], in_=b_psi.rearrange("z (j c) -> (z j) c", c=P))
+        nc.sync.dma_start(out=rows[32:40, :], in_=b_gamma.rearrange("(j c) -> j c", c=P))
+        nc.sync.dma_start(out=rows[40:44, :], in_=beta.rearrange("(j c) -> j c", c=P))
+        phi_dram = phi.rearrange("(t p) d -> p t d", p=P)
+        for h in range(2):
+            nc.sync.dma_start(out=phi_sb[:, :, h * 512 : (h + 1) * 512], in_=phi_dram[:, :, h * 512 : (h + 1) * 512])
+        for z in range(1, Z):
+            load_words(psi_w[z], psi_words[:, :, 2 * D * z : 2 * D * (z + 1)])
+        load_scales(pref_sc, pref_scales)
+        load_words(pref_w, pref_words)
+
+        xg = [w4([P, M, 4], BF16, "xg%d" % g) for g in range(G)]
+        xc = [keep.tile([P, M], U32, name="xc%d" % g, align_bytes=64) for g in range(G)]
+        xs = [keep.tile([P, M], U8, name="xs%d" % g, align_bytes=64) for g in range(G)]
+        xw = []
+        for mt in range(MT):
+            xw_t = work.tile([P, K], BF16, name="xw", tag="xw", bufs=4)
+            if mt % 2 == 0:
+                nc.scalar.copy(out=xw_t[:], in_=xb[mt][:].bitcast(FP8))
+            else:
+                nc.vector.tensor_copy(out=xw_t[:], in_=xb[mt][:].bitcast(FP8))
+            xw.append(xw_t)
+        for mt in range(MT):
+            words = xw[mt][:].bitcast(F32)
+            bank = psum.tile([P, G, 2, P], F32, name="xbank", tag="tr")
+            for g in range(G):
+                for u in range(2):
+                    nc.tensor.transpose(bank[:, g, u, :], words[:, 256 * g + u : 256 * (g + 1) : 2], ident_f[:])
+            for g in range(G):
+                nc.vector.tensor_tensor(
+                    out=xg[g][:, mt * P : (mt + 1) * P, :].rearrange("p r (u e) -> p r u e", u=2),
+                    in0=bank[:, g, :, :].bitcast(BF16).rearrange("p u (r e) -> p r u e", e=2),
+                    in1=x_sc[:, g, :].rearrange("p (u e) -> p u e", u=2).unsqueeze(1).to_broadcast([P, P, 2, 2]),
+                    op=ALU.mult,
+                )
+        for g in range(G):
+            nc.vector.quantize_mx(
+                out=xc[g][:].bitcast(E4X4), scales=xs[g][:], in_=xg[g][:].rearrange("p r t -> p (r t)")
+            )
+
+        cst = keep.tile([P, P], F32, name="cst")
+        cbank = psum.tile([P, P], BF16, name="cbank", tag="tr")
+        nc.tensor.transpose(cbank[:], rows[:], ident_b[:])
+        nc.scalar.copy(out=cst[:], in_=cbank[:])
+
+        phi_t = keep.tile([P, DT, M], BF16, name="phi_t")
+
+        def turn_phi(jd):
+            pbank = psum.tile([P, MT, P], BF16, name="pbank", tag="tr")
+            for mt in range(MT):
+                nc.tensor.transpose(pbank[:, mt, :], phi_sb[:, mt, jd * P : (jd + 1) * P], ident_b[:])
+            nc.scalar.copy(out=phi_t[:, jd, :], in_=pbank[:].rearrange("p t c -> p (t c)"))
+
+        gam = [keep.tile([P, M], F32, name="gam%d" % jd) for jd in range(DT)]
+        pc = {}
+        ps = {}
+        u_tiles = {}
+        psi_tiles = {}
+        y_tiles = {}
+        grouped = {}
+
+        def product(out, w, sc_ap, jd, s_lo):
+            for g in range(G):
+                nc.tensor.matmul_mx(
+                    out=out,
+                    lhsT=w[:, g, 2 * P * jd : 2 * P * (jd + 1)].bitcast(E2X4),
+                    lhsT_scale=sc_ap[:, g, s_lo + P * jd : s_lo + P * (jd + 1)],
+                    rhs=xc[g][:].bitcast(E4X4),
+                    rhs_scale=xs[g][:],
+                    start=(g == 0),
+                    stop=(g == G - 1),
+                )
+
+        def stage_a(s):
+            z, g = s // 2, s % 2
+            for jj in range(4):
+                jd = 4 * g + jj
+                if z == 0:
+                    acc = psum.tile([P, M], F32, name="acc", tag="mm")
+                    product(acc[:], gam_w, gam_sc, jd, 0)
+                    nc.scalar.activation(out=gam[jd][:], in_=acc[:], func=ACT.Sigmoid, bias=cst[:, 32 + jd : 33 + jd])
+                acc = psum.tile([P, M], F32, name="acc", tag="mm")
+                product(acc[:], psi_w[z], psi_sc, jd, z * D)
+                if jj % 2 == 0:
+                    u_tiles[s, jj // 2] = w4([P, 2, M], F32, "u")
+                nc.vector.scalar_tensor_tensor(
+                    out=u_tiles[s, jj // 2][:, jj % 2, :], in0=acc[:],
+                    scalar=cst[:, z * DT + jd : z * DT + jd + 1], in1=gam[jd][:],
+                    op0=ALU.add, op1=ALU.mult,
+                )
+
+        def stage_c(s):
+            g = s % 2
+            for pair in range(2):
+                psi = work.tile([P, 2, M], BF16, name="psi", tag="psi", bufs=3)
+                jd = 4 * g + 2 * pair
+                nc.vector.scalar_tensor_tensor(
+                    out=psi[:], in0=u_tiles.pop((s, pair))[:], scalar=0.0, in1=phi_t[:, jd : jd + 2, :],
+                    op0=ALU.max, op1=ALU.add,
+                )
+                psi_tiles[s, pair] = psi
+
+        def turn_1(s):
+            y = w4([P, MT, 2, P], F32, "y")
+            y_tiles[s] = y
+            for pair in range(2):
+                psi = psi_tiles.pop((s, pair))
+                bank = psum.tile([P, MT, 2, P], BF16, name="t1bank", tag="tr")
+                for ji in range(2):
+                    for mc in range(MT):
+                        nc.tensor.transpose(bank[:, mc, ji, :], psi[:, ji, mc * P : (mc + 1) * P], ident_b[:])
+                src = bank[:].rearrange("p c j d -> p (c j d)").bitcast(F32)
+                nc.scalar.copy(
+                    out=y[:, :, :, 64 * pair : 64 * pair + 64],
+                    in_=src.rearrange("p (c q u) -> p c u q", c=MT, u=2),
+                )
+
+        def turn_2(s):
+            y = y_tiles.pop(s)
+            grp = w4([P, M, 4], BF16, "grp")
+            grouped[s] = grp
+            for cp in range(2):
+                bank = psum.tile([P, 2, 2, P], F32, name="t2bank", tag="tr")
+                for ci in range(2):
+                    for u in range(2):
+                        nc.tensor.transpose(bank[:, ci, u, :], y[:, 2 * cp + ci, u, :], ident_f[:])
+                dst = grp[:, 256 * cp : 256 * (cp + 1), :].rearrange("p r t -> p (r t)").bitcast(F32)
+                nc.scalar.copy(
+                    out=dst.rearrange("p (c r u) -> p c r u", c=2, u=2),
+                    in_=bank[:].rearrange("p c u r -> p c r u"),
+                )
+
+        def stage_q(s):
+            pc[s] = keep.tile([P, M], U32, name="pc%d" % s, align_bytes=64)
+            ps[s] = keep.tile([P, M], U8, name="ps%d" % s, align_bytes=64)
+            nc.vector.quantize_mx(
+                out=pc[s][:].bitcast(E4X4), scales=ps[s][:], in_=grouped.pop(s)[:].rearrange("p r t -> p (r t)")
+            )
+
+        steps = Z * G
+        for s in range(steps + 1):
+            if s < steps:
+                stage_a(s)
+            if s < 2:
+                for jj in range(4):
+                    turn_phi(4 * s + jj)
+            if s >= 1:
+                turn_1(s - 1)
+                turn_2(s - 1)
+            if s < steps:
+                stage_c(s)
+            if s >= 1:
+                stage_q(s - 1)
+
+        best = [keep.tile([P, M], F32, name="best%d" % j) for j in range(TT)]
+        den = keep.tile([P, TT, M], F32, name="den")
+        num = [keep.tile([P, M], F32, name="num%d" % j) for j in range(TT)]
+        out0 = out_0.rearrange("(c p) j -> p c j", p=P)
+        out1 = out_1.rearrange("(c p) j -> p c j", p=P)
+        vals = {}
+        e_tiles = {}
+        ev_tiles = {}
+
+        def values(jt, tag):
+            for z in range(Z):
+                a = psum.tile([P, M], F32, name="val", tag=tag)
+                for g in range(G):
+                    nc.tensor.matmul_mx(
+                        out=a[:],
+                        lhsT=pref_w[:, g, 2 * P * jt : 2 * P * (jt + 1)].bitcast(E2X4),
+                        lhsT_scale=pref_sc[:, g, P * jt : P * (jt + 1)],
+                        rhs=pc[G * z + g][:].bitcast(E4X4),
+                        rhs_scale=ps[G * z + g][:],
+                        start=(g == 0),
+                        stop=(g == G - 1),
+                    )
+                vals[jt, z] = a
+
+        def weights(jt):
+            v0 = work.tile([P, M], F32, name="v0", tag="v0")
+            nc.scalar.copy(out=v0[:], in_=vals[jt, 0][:])
+            m1 = work.tile([P, M], F32, name="m1", tag="m1")
+            m2 = work.tile([P, M], F32, name="m2", tag="m2")
+            nc.vector.tensor_tensor(out=m1[:], in0=v0[:], in1=vals[jt, 1][:], op=ALU.max)
+            nc.vector.tensor_tensor(out=m2[:], in0=m1[:], in1=vals[jt, 2][:], op=ALU.max)
+            nc.vector.tensor_tensor(out=best[jt][:], in0=m2[:], in1=vals[jt, 3][:], op=ALU.max)
+            for zp in range(2):
+                e_tiles[jt, zp] = w4([P, 2, M], F32, "e")
+            for z in range(Z):
+                e = e_tiles[jt, z // 2][:, z % 2, :]
+                nc.vector.tensor_tensor(out=e, in0=vals[jt, z][:], in1=best[jt][:], op=ALU.subtract)
+                nc.scalar.activation(out=e, in_=e, func=ACT.Exp, scale=cst[:, 40 + jt : 41 + jt])
+
+        def weighted(jt):
+            for zp in range(2):
+                ev_tiles[jt, zp] = w4([P, 2, M], F32, "ev")
+            for z in range(Z):
+                nc.vector.tensor_tensor(
+                    out=ev_tiles[jt, z // 2][:, z % 2, :], in0=e_tiles[jt, z // 2][:, z % 2, :],
+                    in1=vals[jt, z][:], op=ALU.mult,
+                )
+
+        def add_up(eng, tiles, jt, out):
+            s = w4([P, 2, M], F32, "s")
+            eng.tensor_tensor(out=s[:], in0=tiles[jt, 0][:], in1=tiles[jt, 1][:], op=ALU.add)
+            eng.tensor_tensor(out=out, in0=s[:, 0, :], in1=s[:, 1, :], op=ALU.add)
+
+        def turn_out(src):
+            bank = psum.tile([P, MT, P], F32, name="obank", tag="tr")
+            for mc in range(MT):
+                nc.tensor.transpose(bank[:, mc, :], src[:, mc * P : (mc + 1) * P], ident_f[:])
+            return bank
+
+        def emit(bank, dram, jt, copy):
+            ob = work.tile([P, MT, P], F32, name="ob", tag="ob", bufs=4)
+            copy(out=ob[:], in_=bank[:])
+            nc.sync.dma_start(out=dram[:, :, jt * P : (jt + 1) * P], in_=ob[:])
+
+        for jt in range(2):
+            values(jt, "mm")
+            weights(jt)
+            add_up(nc.gpsimd, e_tiles, jt, den[:, jt, :])
+            weighted(jt)
+            add_up(nc.gpsimd, ev_tiles, jt, num[jt][:])
+            emit(turn_out(best[jt]), out0, jt, nc.scalar.copy)
+        values(2, "mm")
+        values(3, "tr")
+        weights(2)
+        add_up(nc.gpsimd, e_tiles, 2, den[:, 2, :])
+        weights(3)
+        add_up(nc.gpsimd, e_tiles, 3, den[:, 3, :])
+        weighted(2)
+        add_up(nc.vector, ev_tiles, 2, num[2][:])
+        weighted(3)
+        add_up(nc.vector, ev_tiles, 3, num[3][:])
+        for jt in range(TT):
+            nc.scalar.activation(out=den[:, jt, :], in_=den[:, jt, :], func=ACT.Ln)
+        banks = [turn_out(best[jt]) for jt in (2, 3)]
+        order = (0, 1, 2, 3)
+        for jt in order:
+            nc.scalar.activation(out=den[:, jt, :], in_=den[:, jt, :], func=ACT.Exp, scale=-1.0)
+        for jt in (2, 3):
+            emit(banks[jt - 2], out0, jt, nc.scalar.copy)
+        for jt in order:
+            soft = work.tile([P, M], F32, name="soft", tag="soft", bufs=2)
+            (nc.vector if jt >= 2 else nc.gpsimd).tensor_tensor(out=soft[:], in0=num[jt][:], in1=den[:, jt, :], op=ALU.mult)
+            emit(turn_out(soft), out1, jt, nc.vector.tensor_copy if jt == 3 else nc.scalar.copy)

@@ -39,7 +39,7 @@ def tile_successor_feature_gpi_f1_kernel(
             return work.tile(shape, dtype, name=name, tag="w4", bufs=15, align_bytes=64)
 
         x_sc = keep.tile([P, G, 4], F32, name="x_sc")
-        nc.scalar.dma_start(out=x_sc[:], in_=x_scale.rearrange("o (g p t) -> p (o g) t", g=G, p=P, t=4))
+        nc.gpsimd.dma_start(out=x_sc[:], in_=x_scale.rearrange("o (g p t) -> p (o g) t", g=G, p=P, t=4))
         xb = []
         for mt in range(MT):
             xb_t = keep.tile([P, K], U8, name="xb%d" % mt)
@@ -51,11 +51,16 @@ def tile_successor_feature_gpi_f1_kernel(
         ident_b = keep.tile([P, P], BF16, name="ident_b")
         rows = keep.tile([P, P], BF16, name="rows")
         gam_sc = keep.tile([P, G, D], U8, name="gam_sc", align_bytes=64)
-        psi_sc = keep.tile([P, G, Z * D], U8, name="psi_sc", align_bytes=64)
+        psi_sc0 = keep.tile([P, G, D], U8, name="psi_sc0", align_bytes=64)
+        psi_sc1 = keep.tile([P, G, (Z - 1) * D], U8, name="psi_sc1", align_bytes=64)
         pref_sc = keep.tile([P, G, T], U8, name="pref_sc", align_bytes=64)
         nc.vector.memset(gam_sc[:].rearrange("p g n -> p (g n)").bitcast(I32), 0)
         nc.gpsimd.memset(rows[:], 0.0)
-        nc.gpsimd.memset(psi_sc[:].rearrange("p g n -> p (g n)").bitcast(I32), 0)
+        nc.gpsimd.dma_start(out=rows[0:32, :], in_=b_psi.rearrange("z (j c) -> (z j) c", c=P))
+        nc.gpsimd.dma_start(out=rows[32:40, :], in_=b_gamma.rearrange("(j c) -> j c", c=P))
+        nc.gpsimd.dma_start(out=rows[40:44, :], in_=beta.rearrange("(j c) -> j c", c=P))
+        nc.vector.memset(psi_sc0[:].rearrange("p g n -> p (g n)").bitcast(I32), 0)
+        nc.gpsimd.memset(psi_sc1[:].rearrange("p g n -> p (g n)").bitcast(I32), 0)
         nc.gpsimd.memset(pref_sc[:].rearrange("p g n -> p (g n)").bitcast(I32), 0)
         nc.vector.tensor_copy(out=ident_b[:], in_=ident_f[:])
         warm = keep.tile([P, 1], F32, name="warm")
@@ -74,22 +79,21 @@ def tile_successor_feature_gpi_f1_kernel(
         phi_sb = keep.tile([P, MT, D], BF16, name="phi_sb")
 
         def load_words(tile, dram):
-            nc.sync.dma_start(out=tile[:].bitcast(I32), in_=dram.rearrange("g p b -> p g b").bitcast(I32))
+            nc.sync.dma_start(out=tile.bitcast(I32), in_=dram.rearrange("g p b -> p g b").bitcast(I32))
 
-        load_scales(gam_sc, gamma_scales)
-        load_scales(psi_sc, psi_scales)
-        load_words(gam_w, gamma_words)
-        load_words(psi_w[0], psi_words[:, :, 0 : 2 * D])
-        nc.sync.dma_start(out=rows[0:32, :], in_=b_psi.rearrange("z (j c) -> (z j) c", c=P))
-        nc.sync.dma_start(out=rows[32:40, :], in_=b_gamma.rearrange("(j c) -> j c", c=P))
-        nc.sync.dma_start(out=rows[40:44, :], in_=beta.rearrange("(j c) -> j c", c=P))
         phi_dram = phi.rearrange("(t p) d -> p t d", p=P)
         for h in range(2):
-            nc.sync.dma_start(out=phi_sb[:, :, h * 512 : (h + 1) * 512], in_=phi_dram[:, :, h * 512 : (h + 1) * 512])
+            load_words(gam_w[:, :, h * D : (h + 1) * D], gamma_words[:, :, h * D : (h + 1) * D])
+            load_words(psi_w[0][:, :, h * D : (h + 1) * D], psi_words[:, :, h * D : (h + 1) * D])
+            if h == 0:
+                load_scales(gam_sc, gamma_scales)
+                load_scales(psi_sc0, psi_scales[:, :, 0:D])
+            nc.gpsimd.dma_start(out=phi_sb[:, :, h * 512 : (h + 1) * 512], in_=phi_dram[:, :, h * 512 : (h + 1) * 512])
+        load_scales(psi_sc1, psi_scales[:, :, D : Z * D])
         for z in range(1, Z):
-            load_words(psi_w[z], psi_words[:, :, 2 * D * z : 2 * D * (z + 1)])
+            load_words(psi_w[z][:], psi_words[:, :, 2 * D * z : 2 * D * (z + 1)])
         load_scales(pref_sc, pref_scales)
-        load_words(pref_w, pref_words)
+        load_words(pref_w[:], pref_words)
 
         xg = [w4([P, M, 4], BF16, "xg%d" % g) for g in range(G)]
         xc = [keep.tile([P, M], U32, name="xc%d" % g, align_bytes=64) for g in range(G)]
@@ -97,7 +101,7 @@ def tile_successor_feature_gpi_f1_kernel(
         xw = []
         for mt in range(MT):
             xw_t = work.tile([P, K], BF16, name="xw", tag="xw", bufs=4)
-            if mt % 2 == 0:
+            if mt != 1:
                 nc.scalar.copy(out=xw_t[:], in_=xb[mt][:].bitcast(FP8))
             else:
                 nc.vector.tensor_copy(out=xw_t[:], in_=xb[mt][:].bitcast(FP8))
@@ -153,34 +157,55 @@ def tile_successor_feature_gpi_f1_kernel(
                     stop=(g == G - 1),
                 )
 
-        def stage_a(s):
-            z, g = s // 2, s % 2
+        order = [(0, 0), (1, 0), (0, 1), (1, 1), (2, 0), (2, 1), (3, 0), (3, 1)]
+
+        def discount(jd):
+            acc = psum.tile([P, M], F32, name="acc", tag="mm")
+            product(acc[:], gam_w, gam_sc, jd, 0)
+            nc.scalar.activation(out=gam[jd][:], in_=acc[:], func=ACT.Sigmoid, bias=cst[:, 32 + jd : 33 + jd])
+
+        def feed(s):
+            z, g = order[s]
+            accs = []
             for jj in range(4):
                 jd = 4 * g + jj
-                if z == 0:
-                    acc = psum.tile([P, M], F32, name="acc", tag="mm")
-                    product(acc[:], gam_w, gam_sc, jd, 0)
-                    nc.scalar.activation(out=gam[jd][:], in_=acc[:], func=ACT.Sigmoid, bias=cst[:, 32 + jd : 33 + jd])
+                if s == 0:
+                    discount(jd)
+                if (s, jj) in ((1, 1), (1, 3), (2, 1), (2, 3)):
+                    discount(2 * s + 2 + (jj + 1) // 2 - 1)
                 acc = psum.tile([P, M], F32, name="acc", tag="mm")
-                product(acc[:], psi_w[z], psi_sc, jd, z * D)
-                if jj % 2 == 0:
-                    u_tiles[s, jj // 2] = w4([P, 2, M], F32, "u")
+                product(acc[:], psi_w[z], psi_sc1 if z else psi_sc0, jd, (z - 1) * D if z else 0)
+                accs.append(acc)
+                if jj % 2 == 1:
+                    if s == 0:
+                        turn_phi(jj - 1)
+                        turn_phi(jj)
+                    elif s == 1:
+                        turn_phi(4 + jj - 1)
+                        turn_phi(4 + jj)
+                    gate(s, jj // 2, accs[jj - 1 : jj + 1])
+
+        def gate(s, pair, accs):
+            z, g = order[s]
+            u = w4([P, 2, M], F32, "u")
+            u_tiles[s, pair] = u
+            for ji in range(2):
+                jd = 4 * g + 2 * pair + ji
                 nc.vector.scalar_tensor_tensor(
-                    out=u_tiles[s, jj // 2][:, jj % 2, :], in0=acc[:],
-                    scalar=cst[:, z * DT + jd : z * DT + jd + 1], in1=gam[jd][:],
+                    out=u[:, ji, :], in0=accs[ji][:], scalar=cst[:, z * DT + jd : z * DT + jd + 1], in1=gam[jd][:],
                     op0=ALU.add, op1=ALU.mult,
                 )
+                if pair == 1 and ji == 0:
+                    combine(s, 0)
 
-        def stage_c(s):
-            g = s % 2
-            for pair in range(2):
-                psi = work.tile([P, 2, M], BF16, name="psi", tag="psi", bufs=3)
-                jd = 4 * g + 2 * pair
-                nc.vector.scalar_tensor_tensor(
-                    out=psi[:], in0=u_tiles.pop((s, pair))[:], scalar=0.0, in1=phi_t[:, jd : jd + 2, :],
-                    op0=ALU.max, op1=ALU.add,
-                )
-                psi_tiles[s, pair] = psi
+        def combine(s, pair):
+            psi = work.tile([P, 2, M], BF16, name="psi", tag="psi", bufs=3)
+            jd = 4 * order[s][1] + 2 * pair
+            nc.vector.scalar_tensor_tensor(
+                out=psi[:], in0=u_tiles.pop((s, pair))[:], scalar=0.0, in1=phi_t[:, jd : jd + 2, :],
+                op0=ALU.max, op1=ALU.add,
+            )
+            psi_tiles[s, pair] = psi
 
         def turn_1(s):
             y = w4([P, MT, 2, P], F32, "y")
@@ -207,123 +232,172 @@ def tile_successor_feature_gpi_f1_kernel(
                     for u in range(2):
                         nc.tensor.transpose(bank[:, ci, u, :], y[:, 2 * cp + ci, u, :], ident_f[:])
                 dst = grp[:, 256 * cp : 256 * (cp + 1), :].rearrange("p r t -> p (r t)").bitcast(F32)
-                nc.scalar.copy(
+                copy = nc.vector.tensor_copy if s == steps - 1 and cp == 1 else nc.scalar.copy
+                copy(
                     out=dst.rearrange("p (c r u) -> p c r u", c=2, u=2),
                     in_=bank[:].rearrange("p c u r -> p c r u"),
                 )
 
         def stage_q(s):
-            pc[s] = keep.tile([P, M], U32, name="pc%d" % s, align_bytes=64)
-            ps[s] = keep.tile([P, M], U8, name="ps%d" % s, align_bytes=64)
+            pc[order[s]] = keep.tile([P, M], U32, name="pc%d" % s, align_bytes=64)
+            ps[order[s]] = keep.tile([P, M], U8, name="ps%d" % s, align_bytes=64)
             nc.vector.quantize_mx(
-                out=pc[s][:].bitcast(E4X4), scales=ps[s][:], in_=grouped.pop(s)[:].rearrange("p r t -> p (r t)")
+                out=pc[order[s]][:].bitcast(E4X4), scales=ps[order[s]][:], in_=grouped.pop(s)[:].rearrange("p r t -> p (r t)")
             )
 
         steps = Z * G
-        for s in range(steps + 1):
-            if s < steps:
-                stage_a(s)
-            if s < 2:
-                for jj in range(4):
-                    turn_phi(4 * s + jj)
-            if s >= 1:
-                turn_1(s - 1)
-                turn_2(s - 1)
-            if s < steps:
-                stage_c(s)
-            if s >= 1:
-                stage_q(s - 1)
+        vals = {}
+
+        def value(jt, z, tag):
+            a = psum.tile([P, M], F32, name="val", tag=tag)
+            for g in range(G):
+                nc.tensor.matmul_mx(
+                    out=a[:],
+                    lhsT=pref_w[:, g, 2 * P * jt : 2 * P * (jt + 1)].bitcast(E2X4),
+                    lhsT_scale=pref_sc[:, g, P * jt : P * (jt + 1)],
+                    rhs=pc[z, g][:].bitcast(E4X4),
+                    rhs_scale=ps[z, g][:],
+                    start=(g == 0),
+                    stop=(g == G - 1),
+                )
+            vals[jt, z] = a
 
         best = [keep.tile([P, M], F32, name="best%d" % j) for j in range(TT)]
         den = keep.tile([P, TT, M], F32, name="den")
-        num = [keep.tile([P, M], F32, name="num%d" % j) for j in range(TT)]
+        num = [keep.tile([P, M], F32, name="num%d" % j) for j in range(TT - 1)]
         out0 = out_0.rearrange("(c p) j -> p c j", p=P)
         out1 = out_1.rearrange("(c p) j -> p c j", p=P)
-        vals = {}
         e_tiles = {}
         ev_tiles = {}
+        part = {}
 
-        def values(jt, tag):
-            for z in range(Z):
-                a = psum.tile([P, M], F32, name="val", tag=tag)
-                for g in range(G):
-                    nc.tensor.matmul_mx(
-                        out=a[:],
-                        lhsT=pref_w[:, g, 2 * P * jt : 2 * P * (jt + 1)].bitcast(E2X4),
-                        lhsT_scale=pref_sc[:, g, P * jt : P * (jt + 1)],
-                        rhs=pc[G * z + g][:].bitcast(E4X4),
-                        rhs_scale=ps[G * z + g][:],
-                        start=(g == 0),
-                        stop=(g == G - 1),
-                    )
-                vals[jt, z] = a
-
-        def weights(jt):
+        def save_first(jt):
             v0 = work.tile([P, M], F32, name="v0", tag="v0")
             nc.scalar.copy(out=v0[:], in_=vals[jt, 0][:])
-            m1 = work.tile([P, M], F32, name="m1", tag="m1")
-            m2 = work.tile([P, M], F32, name="m2", tag="m2")
-            nc.vector.tensor_tensor(out=m1[:], in0=v0[:], in1=vals[jt, 1][:], op=ALU.max)
-            nc.vector.tensor_tensor(out=m2[:], in0=m1[:], in1=vals[jt, 2][:], op=ALU.max)
-            nc.vector.tensor_tensor(out=best[jt][:], in0=m2[:], in1=vals[jt, 3][:], op=ALU.max)
-            for zp in range(2):
-                e_tiles[jt, zp] = w4([P, 2, M], F32, "e")
-            for z in range(Z):
-                e = e_tiles[jt, z // 2][:, z % 2, :]
-                nc.vector.tensor_tensor(out=e, in0=vals[jt, z][:], in1=best[jt][:], op=ALU.subtract)
-                nc.scalar.activation(out=e, in_=e, func=ACT.Exp, scale=cst[:, 40 + jt : 41 + jt])
+            part[jt] = v0
 
-        def weighted(jt):
-            for zp in range(2):
-                ev_tiles[jt, zp] = w4([P, 2, M], F32, "ev")
-            for z in range(Z):
-                nc.vector.tensor_tensor(
-                    out=ev_tiles[jt, z // 2][:, z % 2, :], in0=e_tiles[jt, z // 2][:, z % 2, :],
-                    in1=vals[jt, z][:], op=ALU.mult,
-                )
+        def larger(jt, z):
+            if z < Z - 1:
+                m = work.tile([P, M], F32, name="m%d" % z, tag="m%d" % z)
+            else:
+                m = best[jt]
+            nc.vector.tensor_tensor(out=m[:], in0=part[jt][:], in1=vals[jt, z][:], op=ALU.max)
+            part[jt] = m
 
-        def add_up(eng, tiles, jt, out):
+        def weight(jt, z):
+            if z % 2 == 0:
+                e_tiles[jt, z // 2] = w4([P, 2, M], F32, "e")
+            e = e_tiles[jt, z // 2][:, z % 2, :]
+            nc.vector.tensor_tensor(out=e, in0=vals[jt, z][:], in1=best[jt][:], op=ALU.subtract)
+            nc.scalar.activation(out=e, in_=e, func=ACT.Exp, scale=cst[:, 40 + jt : 41 + jt])
+
+        def weigh(jt, z):
+            if z % 2 == 0:
+                ev_tiles[jt, z // 2] = w4([P, 2, M], F32, "ev")
+            nc.vector.tensor_tensor(
+                out=ev_tiles[jt, z // 2][:, z % 2, :], in0=e_tiles[jt, z // 2][:, z % 2, :],
+                in1=vals[jt, z][:], op=ALU.mult,
+            )
+
+        def add_pairs(eng, tiles, jt):
             s = w4([P, 2, M], F32, "s")
             eng.tensor_tensor(out=s[:], in0=tiles[jt, 0][:], in1=tiles[jt, 1][:], op=ALU.add)
+            return s
+
+        def add_halves(eng, s, out):
             eng.tensor_tensor(out=out, in0=s[:, 0, :], in1=s[:, 1, :], op=ALU.add)
 
-        def turn_out(src):
-            bank = psum.tile([P, MT, P], F32, name="obank", tag="tr")
+        def add_up(eng, tiles, jt, out):
+            add_halves(eng, add_pairs(eng, tiles, jt), out)
+
+        def turn_out(src, tag):
+            bank = psum.tile([P, MT, P], F32, name="obank", tag=tag)
             for mc in range(MT):
                 nc.tensor.transpose(bank[:, mc, :], src[:, mc * P : (mc + 1) * P], ident_f[:])
             return bank
 
         def emit(bank, dram, jt, copy):
-            ob = work.tile([P, MT, P], F32, name="ob", tag="ob", bufs=4)
+            ob = work.tile([P, MT, P], F32, name="ob", tag="ob", bufs=8)
             copy(out=ob[:], in_=bank[:])
             nc.sync.dma_start(out=dram[:, :, jt * P : (jt + 1) * P], in_=ob[:])
 
-        for jt in range(2):
-            values(jt, "mm")
-            weights(jt)
-            add_up(nc.gpsimd, e_tiles, jt, den[:, jt, :])
-            weighted(jt)
-            add_up(nc.gpsimd, ev_tiles, jt, num[jt][:])
-            emit(turn_out(best[jt]), out0, jt, nc.scalar.copy)
-        values(2, "mm")
-        values(3, "tr")
-        weights(2)
+        for s in range(steps):
+            feed(s)
+            combine(s, 1)
+            if s >= 1:
+                turn_1(s - 1)
+                turn_2(s - 1)
+                stage_q(s - 1)
+        for z in range(Z - 1):
+            value(0, z, "mm")
+        save_first(0)
+        larger(0, 1)
+        larger(0, 2)
+        turn_1(steps - 1)
+        turn_2(steps - 1)
+        stage_q(steps - 1)
+
+        def total(tiles, jt):
+            bank = psum.tile([P, M], F32, name="sum", tag="mm")
+            for z in range(Z):
+                nc.tensor.matmul(bank[:], ident_f[:], tiles[jt, z // 2][:, z % 2, :], start=(z == 0), stop=(z == Z - 1))
+            return bank
+
+        value(0, 3, "mm")
+        for z in range(Z):
+            value(1, z, "tr")
+        save_first(1)
+        larger(0, 3)
+        for z in range(Z):
+            weight(0, z)
+        add_up(nc.gpsimd, e_tiles, 0, den[:, 0, :])
+        for z in range(Z):
+            weigh(0, z)
+            if z < Z - 1:
+                larger(1, z + 1)
+        bank = turn_out(best[0], "mm")
+        emit(bank, out0, 0, nc.scalar.copy)
+        add_up(nc.gpsimd, ev_tiles, 0, num[0][:])
+        for z in range(Z):
+            value(2, z, "mm")
+        save_first(2)
+        for z in range(Z):
+            weight(1, z)
+        add_up(nc.gpsimd, e_tiles, 1, den[:, 1, :])
+        for z in range(Z):
+            weigh(1, z)
+            if z < Z - 1:
+                larger(2, z + 1)
+        bank = turn_out(best[1], "tr")
+        emit(bank, out0, 1, nc.scalar.copy)
+        half_1 = add_pairs(nc.gpsimd, ev_tiles, 1)
+        for z in range(Z):
+            value(3, z, "tr")
+        save_first(3)
+        for z in range(Z):
+            weight(2, z)
+            if z < Z - 1:
+                larger(3, z + 1)
         add_up(nc.gpsimd, e_tiles, 2, den[:, 2, :])
-        weights(3)
-        add_up(nc.gpsimd, e_tiles, 3, den[:, 3, :])
-        weighted(2)
-        add_up(nc.vector, ev_tiles, 2, num[2][:])
-        weighted(3)
-        add_up(nc.vector, ev_tiles, 3, num[3][:])
+        for z in range(Z):
+            weight(3, z)
+        add_halves(nc.gpsimd, half_1, num[1][:])
+        for z in range(Z):
+            weigh(2, z)
+        den_3 = total(e_tiles, 3)
         for jt in range(TT):
-            nc.scalar.activation(out=den[:, jt, :], in_=den[:, jt, :], func=ACT.Ln)
-        banks = [turn_out(best[jt]) for jt in (2, 3)]
-        order = (0, 1, 2, 3)
-        for jt in order:
+            nc.scalar.activation(out=den[:, jt, :], in_=den[:, jt, :] if jt < 3 else den_3[:], func=ACT.Ln)
+        for jt in range(TT):
             nc.scalar.activation(out=den[:, jt, :], in_=den[:, jt, :], func=ACT.Exp, scale=-1.0)
+        for z in range(Z):
+            weigh(3, z)
+        num_3 = total(ev_tiles, 3)
+        banks = {2: turn_out(best[2], "mm"), 3: turn_out(best[3], "mm")}
+        add_up(nc.vector, ev_tiles, 2, num[2][:])
+        for jt in range(TT):
+            soft = work.tile([P, M], F32, name="soft", tag="soft", bufs=4)
+            nc.vector.tensor_tensor(out=soft[:], in0=num[jt][:] if jt < 3 else num_3[:], in1=den[:, jt, :], op=ALU.mult)
+            bank = turn_out(soft, "mm" if jt % 2 else "tr")
+            emit(bank, out1, jt, nc.vector.tensor_copy if jt == 3 else nc.scalar.copy)
         for jt in (2, 3):
-            emit(banks[jt - 2], out0, jt, nc.scalar.copy)
-        for jt in order:
-            soft = work.tile([P, M], F32, name="soft", tag="soft", bufs=2)
-            (nc.vector if jt >= 2 else nc.gpsimd).tensor_tensor(out=soft[:], in0=num[jt][:], in1=den[:, jt, :], op=ALU.mult)
-            emit(turn_out(soft), out1, jt, nc.vector.tensor_copy if jt == 3 else nc.scalar.copy)
+            emit(banks[jt], out0, jt, nc.vector.tensor_copy if jt == 2 else nc.scalar.copy)

@@ -82,18 +82,28 @@ def tile_successor_feature_gpi_f1_kernel(
             nc.sync.dma_start(out=tile.bitcast(I32), in_=dram.rearrange("g p b -> p g b").bitcast(I32))
 
         phi_dram = phi.rearrange("(t p) d -> p t d", p=P)
+        nc.sync.dma_start(out=phi_sb[:, :, 0:512], in_=phi_dram[:, :, 0:512])
         for h in range(2):
             load_words(gam_w[:, :, h * D : (h + 1) * D], gamma_words[:, :, h * D : (h + 1) * D])
             load_words(psi_w[0][:, :, h * D : (h + 1) * D], psi_words[:, :, h * D : (h + 1) * D])
             if h == 0:
                 load_scales(gam_sc, gamma_scales)
                 load_scales(psi_sc0, psi_scales[:, :, 0:D])
-            nc.gpsimd.dma_start(out=phi_sb[:, :, h * 512 : (h + 1) * 512], in_=phi_dram[:, :, h * 512 : (h + 1) * 512])
+            if h == 1:
+                nc.gpsimd.dma_start(out=phi_sb[:, :, 512:], in_=phi_dram[:, :, 512:])
         load_scales(psi_sc1, psi_scales[:, :, D : Z * D])
         for z in range(1, Z):
             load_words(psi_w[z][:], psi_words[:, :, 2 * D * z : 2 * D * (z + 1)])
         load_scales(pref_sc, pref_scales)
         load_words(pref_w[:], pref_words)
+
+        idle = keep.tile([P, M], BF16, name="idle")
+        nc.vector.memset(idle[:], 0.0)
+
+        def keep_clock(count):
+            bank = psum.tile([P, M], F32, name="clock", tag="mm")
+            for i in range(count):
+                nc.tensor.matmul(bank[:], idle[:, 0:P], idle[:], start=True, stop=True)
 
         xg = [w4([P, M, 4], BF16, "xg%d" % g) for g in range(G)]
         xc = [keep.tile([P, M], U32, name="xc%d" % g, align_bytes=64) for g in range(G)]
@@ -106,12 +116,14 @@ def tile_successor_feature_gpi_f1_kernel(
             else:
                 nc.vector.tensor_copy(out=xw_t[:], in_=xb[mt][:].bitcast(FP8))
             xw.append(xw_t)
+        keep_clock(4)
         for mt in range(MT):
             words = xw[mt][:].bitcast(F32)
             bank = psum.tile([P, G, 2, P], F32, name="xbank", tag="tr")
             for g in range(G):
                 for u in range(2):
                     nc.tensor.transpose(bank[:, g, u, :], words[:, 256 * g + u : 256 * (g + 1) : 2], ident_f[:])
+            keep_clock(2)
             for g in range(G):
                 nc.vector.tensor_tensor(
                     out=xg[g][:, mt * P : (mt + 1) * P, :].rearrange("p r (u e) -> p r u e", u=2),
@@ -177,13 +189,12 @@ def tile_successor_feature_gpi_f1_kernel(
                 product(acc[:], psi_w[z], psi_sc1 if z else psi_sc0, jd, (z - 1) * D if z else 0)
                 accs.append(acc)
                 if jj % 2 == 1:
-                    if s == 0:
-                        turn_phi(jj - 1)
-                        turn_phi(jj)
-                    elif s == 1:
+                    if s == 1:
                         turn_phi(4 + jj - 1)
                         turn_phi(4 + jj)
                     gate(s, jj // 2, accs[jj - 1 : jj + 1])
+                    for turn in turns[s, jj // 2]:
+                        turn[0](*turn[1:])
 
         def gate(s, pair, accs):
             z, g = order[s]
@@ -195,30 +206,38 @@ def tile_successor_feature_gpi_f1_kernel(
                     out=u[:, ji, :], in0=accs[ji][:], scalar=cst[:, z * DT + jd : z * DT + jd + 1], in1=gam[jd][:],
                     op0=ALU.add, op1=ALU.mult,
                 )
-                if pair == 1 and ji == 0:
+                if s > 0 and pair == 1 and ji == 0:
                     combine(s, 0)
+            if s == 0 and pair == 0:
+                combine(s, 0)
 
-        def combine(s, pair):
-            psi = work.tile([P, 2, M], BF16, name="psi", tag="psi", bufs=3)
+        def combine(s, pair, parts=1):
+            psi = work.tile([P, 2, M], BF16, name="psi", tag="psi", bufs=5)
             jd = 4 * order[s][1] + 2 * pair
-            nc.vector.scalar_tensor_tensor(
-                out=psi[:], in0=u_tiles.pop((s, pair))[:], scalar=0.0, in1=phi_t[:, jd : jd + 2, :],
-                op0=ALU.max, op1=ALU.add,
-            )
+            u = u_tiles.pop((s, pair))
+            for i in range(parts):
+                lo, hi = 2 * i // parts, 2 * (i + 1) // parts
+                nc.vector.scalar_tensor_tensor(
+                    out=psi[:, lo:hi, :], in0=u[:, lo:hi, :], scalar=0.0, in1=phi_t[:, jd + lo : jd + hi, :],
+                    op0=ALU.max, op1=ALU.add,
+                )
             psi_tiles[s, pair] = psi
 
-        def turn_1(s):
-            y = w4([P, MT, 2, P], F32, "y")
-            y_tiles[s] = y
-            for pair in range(2):
-                psi = psi_tiles.pop((s, pair))
-                bank = psum.tile([P, MT, 2, P], BF16, name="t1bank", tag="tr")
-                for ji in range(2):
+        def turn_1(s, pair, copies=(nc.scalar.copy,)):
+            if pair == 0:
+                y_tiles[s] = w4([P, MT, 2, P], F32, "y")
+            y = y_tiles[s]
+            psi = psi_tiles.pop((s, pair))
+            w = 2 // len(copies)
+            for i, copy in enumerate(copies):
+                bank = psum.tile([P, MT, w, P], BF16, name="t1bank", tag="tr")
+                for ji in range(w):
                     for mc in range(MT):
-                        nc.tensor.transpose(bank[:, mc, ji, :], psi[:, ji, mc * P : (mc + 1) * P], ident_b[:])
+                        nc.tensor.transpose(bank[:, mc, ji, :], psi[:, i * w + ji, mc * P : (mc + 1) * P], ident_b[:])
                 src = bank[:].rearrange("p c j d -> p (c j d)").bitcast(F32)
-                nc.scalar.copy(
-                    out=y[:, :, :, 64 * pair : 64 * pair + 64],
+                lo = 64 * pair + 32 * w * i
+                copy(
+                    out=y[:, :, :, lo : lo + 32 * w],
                     in_=src.rearrange("p (c q u) -> p c u q", c=MT, u=2),
                 )
 
@@ -264,7 +283,7 @@ def tile_successor_feature_gpi_f1_kernel(
 
         best = [keep.tile([P, M], F32, name="best%d" % j) for j in range(TT)]
         den = keep.tile([P, TT, M], F32, name="den")
-        num = [keep.tile([P, M], F32, name="num%d" % j) for j in range(TT - 1)]
+        num = [keep.tile([P, M], F32, name="num%d" % j) for j in range(TT)]
         out0 = out_0.rearrange("(c p) j -> p c j", p=P)
         out1 = out_1.rearrange("(c p) j -> p c j", p=P)
         e_tiles = {}
@@ -307,9 +326,6 @@ def tile_successor_feature_gpi_f1_kernel(
         def add_halves(eng, s, out):
             eng.tensor_tensor(out=out, in0=s[:, 0, :], in1=s[:, 1, :], op=ALU.add)
 
-        def add_up(eng, tiles, jt, out):
-            add_halves(eng, add_pairs(eng, tiles, jt), out)
-
         def turn_out(src, tag):
             bank = psum.tile([P, MT, P], F32, name="obank", tag=tag)
             for mc in range(MT):
@@ -321,83 +337,111 @@ def tile_successor_feature_gpi_f1_kernel(
             copy(out=ob[:], in_=bank[:])
             nc.sync.dma_start(out=dram[:, :, jt * P : (jt + 1) * P], in_=ob[:])
 
+        for jd in range(4):
+            turn_phi(jd)
+            if jd == 1:
+                keep_clock(2)
+        turns = {(s, pair): [] for s in range(steps) for pair in range(2)}
+        for s in range(2, steps):
+            turns[s, 0] = [(turn_1, s - 2, 1)]
+            turns[s, 1] = [(turn_2, s - 2), (turn_1, s - 1, 0)]
+        turns[1, 1] = [(turn_1, 0, 0)]
+        turns[7, 0] = [(turn_1, 5, 1), (turn_1, 6, 0)]
+        turns[7, 1] = [(turn_2, 5), (turn_1, 6, 1)]
         for s in range(steps):
             feed(s)
-            combine(s, 1)
-            if s >= 1:
-                turn_1(s - 1)
-                turn_2(s - 1)
-                stage_q(s - 1)
+            combine(s, 1, parts=2 if s == steps - 1 else 1)
+            if s == 2:
+                nc.scalar.activation(out=warm[:], in_=ident_f[:, 0:1], func=ACT.Exp)
+            if s >= 2:
+                stage_q(s - 2)
         for z in range(Z - 1):
             value(0, z, "mm")
+            if z == 0:
+                turn_2(6)
         save_first(0)
+        turn_1(7, 0)
+        stage_q(6)
         larger(0, 1)
         larger(0, 2)
-        turn_1(steps - 1)
-        turn_2(steps - 1)
-        stage_q(steps - 1)
+        keep_clock(2)
+        turn_1(7, 1, (nc.scalar.copy, nc.vector.tensor_copy))
+        keep_clock(2)
+        turn_2(7)
+        stage_q(7)
 
-        def total(tiles, jt):
-            bank = psum.tile([P, M], F32, name="sum", tag="mm")
-            for z in range(Z):
-                nc.tensor.matmul(bank[:], ident_f[:], tiles[jt, z // 2][:, z % 2, :], start=(z == 0), stop=(z == Z - 1))
-            return bank
+        def add_to(total, tiles, jt, z):
+            if z > 0:
+                first = tiles[jt, 0][:, 0, :] if z == 1 else total
+                nc.gpsimd.tensor_tensor(out=total, in0=first, in1=tiles[jt, z // 2][:, z % 2, :], op=ALU.add)
+
+        def soft_out(jt, tag):
+            soft = work.tile([P, M], F32, name="soft", tag="soft", bufs=4)
+            nc.vector.tensor_tensor(out=soft[:], in0=num[jt][:], in1=den[:, jt, :], op=ALU.mult)
+            return turn_out(soft, tag)
 
         value(0, 3, "mm")
         for z in range(Z):
             value(1, z, "tr")
-        save_first(1)
         larger(0, 3)
         for z in range(Z):
             weight(0, z)
-        add_up(nc.gpsimd, e_tiles, 0, den[:, 0, :])
+            add_to(den[:, 0, :], e_tiles, 0, z)
+            if z == 1:
+                save_first(1)
         for z in range(Z):
             weigh(0, z)
+            add_to(num[0][:], ev_tiles, 0, z)
             if z < Z - 1:
                 larger(1, z + 1)
-        bank = turn_out(best[0], "mm")
-        emit(bank, out0, 0, nc.scalar.copy)
-        add_up(nc.gpsimd, ev_tiles, 0, num[0][:])
+        bank_0 = turn_out(best[0], "mm")
         for z in range(Z):
             value(2, z, "mm")
-        save_first(2)
         for z in range(Z):
             weight(1, z)
-        add_up(nc.gpsimd, e_tiles, 1, den[:, 1, :])
+            add_to(den[:, 1, :], e_tiles, 1, z)
+            if z == 1:
+                save_first(2)
+        emit(bank_0, out0, 0, nc.scalar.copy)
         for z in range(Z):
             weigh(1, z)
+            if z < 2:
+                add_to(num[1][:], ev_tiles, 1, z)
             if z < Z - 1:
                 larger(2, z + 1)
-        bank = turn_out(best[1], "tr")
-        emit(bank, out0, 1, nc.scalar.copy)
-        half_1 = add_pairs(nc.gpsimd, ev_tiles, 1)
+        bank_1 = turn_out(best[1], "tr")
         for z in range(Z):
             value(3, z, "tr")
+        emit(bank_1, out0, 1, nc.scalar.copy)
         save_first(3)
         for z in range(Z):
             weight(2, z)
+            add_to(den[:, 2, :], e_tiles, 2, z)
             if z < Z - 1:
                 larger(3, z + 1)
-        add_up(nc.gpsimd, e_tiles, 2, den[:, 2, :])
         for z in range(Z):
             weight(3, z)
-        add_halves(nc.gpsimd, half_1, num[1][:])
+            add_to(den[:, 3, :], e_tiles, 3, z)
+        for z in range(2, Z):
+            add_to(num[1][:], ev_tiles, 1, z)
         for z in range(Z):
             weigh(2, z)
-        den_3 = total(e_tiles, 3)
-        for jt in range(TT):
-            nc.scalar.activation(out=den[:, jt, :], in_=den[:, jt, :] if jt < 3 else den_3[:], func=ACT.Ln)
-        for jt in range(TT):
-            nc.scalar.activation(out=den[:, jt, :], in_=den[:, jt, :], func=ACT.Exp, scale=-1.0)
+        bank_2 = turn_out(best[2], "mm")
+        bank_3 = turn_out(best[3], "mm")
         for z in range(Z):
             weigh(3, z)
-        num_3 = total(ev_tiles, 3)
-        banks = {2: turn_out(best[2], "mm"), 3: turn_out(best[3], "mm")}
-        add_up(nc.vector, ev_tiles, 2, num[2][:])
-        for jt in range(TT):
-            soft = work.tile([P, M], F32, name="soft", tag="soft", bufs=4)
-            nc.vector.tensor_tensor(out=soft[:], in0=num[jt][:] if jt < 3 else num_3[:], in1=den[:, jt, :], op=ALU.mult)
-            bank = turn_out(soft, "mm" if jt % 2 else "tr")
-            emit(bank, out1, jt, nc.vector.tensor_copy if jt == 3 else nc.scalar.copy)
         for jt in (2, 3):
-            emit(banks[jt], out0, jt, nc.vector.tensor_copy if jt == 2 else nc.scalar.copy)
+            s = add_pairs(nc.vector, ev_tiles, jt)
+            add_halves(nc.vector, s, num[jt][:])
+        for jt in range(TT):
+            if jt == 3:
+                emit(bank_2, out0, 2, nc.scalar.copy)
+                emit(bank_3, out0, 3, nc.scalar.copy)
+            nc.scalar.activation(out=den[:, jt, :], in_=den[:, jt, :], func=ACT.Ln)
+        for jt in (0, 2, 3, 1):
+            nc.scalar.activation(out=den[:, jt, :], in_=den[:, jt, :], func=ACT.Exp, scale=-1.0)
+        softs = [soft_out(jt, "mm" if jt < 2 else "tr") for jt in (0, 2, 3, 1)]
+        emit(softs[0], out1, 0, nc.scalar.copy)
+        emit(softs[1], out1, 2, nc.vector.tensor_copy)
+        emit(softs[2], out1, 3, nc.scalar.copy)
+        emit(softs[3], out1, 1, nc.vector.tensor_copy)

from contextlib import ExitStack

import concourse.mybir as mybir
from concourse.masks import make_identity

F32 = mybir.dt.float32
BF16 = mybir.dt.bfloat16
U8 = mybir.dt.uint8
I32 = mybir.dt.int32
U32 = mybir.dt.uint32
FP8 = mybir.dt.float8_e4m3fn
E4X4 = mybir.dt.float8_e4m3fn_x4
E2X4 = mybir.dt.float4_e2m1fn_x4
ACT = mybir.ActivationFunctionType
ALU = mybir.AluOpType

P = 128
M, K, Z, D, T = 512, 1024, 4, 1024, 512
G = 2
MT = M // P
DT = D // P
TT = T // P

FLOPS = 2 * M * K * (Z * D + D) + 2 * M * Z * D * T


def tile_successor_feature_gpi_f1_kernel(
    tc, x_bytes, x_scale, phi, psi_words, psi_scales, b_psi, gamma_words, gamma_scales,
    b_gamma, pref_words, pref_scales, beta, out_0, out_1,
):
    nc = tc.nc
    with ExitStack() as ctx:
        keep = ctx.enter_context(tc.tile_pool(name="keep", bufs=1))
        work = ctx.enter_context(tc.tile_pool(name="work", bufs=2))
        psum = ctx.enter_context(tc.psum_pool(name="psum", bufs=4))
        ctx.enter_context(tc.manual_schedule())

        def w4(shape, dtype, name):
            return work.tile(shape, dtype, name=name, tag="w4", bufs=15, align_bytes=64)

        x_sc = keep.tile([P, G, 4], F32, name="x_sc")
        nc.gpsimd.dma_start(out=x_sc[:], in_=x_scale.rearrange("o (g p t) -> p (o g) t", g=G, p=P, t=4))
        xb = []
        for mt in range(MT):
            xb_t = keep.tile([P, K], U8, name="xb%d" % mt)
            nc.sync.dma_start(out=xb_t[:], in_=x_bytes[mt * P : (mt + 1) * P, :])
            xb.append(xb_t)

        ident_f = keep.tile([P, P], F32, name="ident_f")
        make_identity(nc, ident_f[:])
        ident_b = keep.tile([P, P], BF16, name="ident_b")
        rows = keep.tile([P, P], BF16, name="rows")
        gam_sc = keep.tile([P, G, D], U8, name="gam_sc", align_bytes=64)
        psi_sc0 = keep.tile([P, G, D], U8, name="psi_sc0", align_bytes=64)
        psi_sc1 = keep.tile([P, G, (Z - 1) * D], U8, name="psi_sc1", align_bytes=64)
        pref_sc = keep.tile([P, G, T], U8, name="pref_sc", align_bytes=64)
        nc.vector.memset(gam_sc[:].rearrange("p g n -> p (g n)").bitcast(I32), 0)
        nc.gpsimd.memset(rows[:], 0.0)
        nc.gpsimd.dma_start(out=rows[0:32, :], in_=b_psi.rearrange("z (j c) -> (z j) c", c=P))
        nc.gpsimd.dma_start(out=rows[32:40, :], in_=b_gamma.rearrange("(j c) -> j c", c=P))
        nc.gpsimd.dma_start(out=rows[40:44, :], in_=beta.rearrange("(j c) -> j c", c=P))
        nc.vector.memset(psi_sc0[:].rearrange("p g n -> p (g n)").bitcast(I32), 0)
        nc.gpsimd.memset(psi_sc1[:].rearrange("p g n -> p (g n)").bitcast(I32), 0)
        nc.gpsimd.memset(pref_sc[:].rearrange("p g n -> p (g n)").bitcast(I32), 0)
        nc.vector.tensor_copy(out=ident_b[:], in_=ident_f[:])
        warm = keep.tile([P, 1], F32, name="warm")
        nc.scalar.activation(out=warm[:], in_=ident_f[:, 0:1], func=ACT.Sigmoid)

        def load_scales(plane, dram):
            for q in range(4):
                nc.sync.dma_start(
                    out=plane[32 * q : 32 * q + 4, :, :].bitcast(I32),
                    in_=dram[:, 4 * q : 4 * q + 4, :].rearrange("g q n -> q g n").bitcast(I32),
                )

        gam_w = keep.tile([P, G, 2 * D], U8, name="gam_w", align_bytes=64)
        psi_w = [keep.tile([P, G, 2 * D], U8, name="psi_w%d" % z, align_bytes=64) for z in range(Z)]
        pref_w = keep.tile([P, G, 2 * T], U8, name="pref_w", align_bytes=64)
        phi_sb = keep.tile([P, MT, D], BF16, name="phi_sb")

        def load_words(tile, dram):
            nc.sync.dma_start(out=tile.bitcast(I32), in_=dram.rearrange("g p b -> p g b").bitcast(I32))

        phi_dram = phi.rearrange("(t p) d -> p t d", p=P)
        nc.sync.dma_start(out=phi_sb[:, :, 0:512], in_=phi_dram[:, :, 0:512])
        for h in range(2):
            load_words(gam_w[:, :, h * D : (h + 1) * D], gamma_words[:, :, h * D : (h + 1) * D])
            load_words(psi_w[0][:, :, h * D : (h + 1) * D], psi_words[:, :, h * D : (h + 1) * D])
            if h == 0:
                load_scales(gam_sc, gamma_scales)
                load_scales(psi_sc0, psi_scales[:, :, 0:D])
            if h == 1:
                nc.gpsimd.dma_start(out=phi_sb[:, :, 512:], in_=phi_dram[:, :, 512:])
        load_scales(psi_sc1, psi_scales[:, :, D : Z * D])
        for z in range(1, Z):
            load_words(psi_w[z][:], psi_words[:, :, 2 * D * z : 2 * D * (z + 1)])
        load_scales(pref_sc, pref_scales)
        load_words(pref_w[:], pref_words)

        idle = keep.tile([P, M], BF16, name="idle")
        nc.vector.memset(idle[:], 0.0)

        def keep_clock(count):
            bank = psum.tile([P, M], F32, name="clock", tag="mm")
            for i in range(count):
                nc.tensor.matmul(bank[:], idle[:, 0:P], idle[:], start=True, stop=True)

        xg = [w4([P, M, 4], BF16, "xg%d" % g) for g in range(G)]
        xc = [keep.tile([P, M], U32, name="xc%d" % g, align_bytes=64) for g in range(G)]
        xs = [keep.tile([P, M], U8, name="xs%d" % g, align_bytes=64) for g in range(G)]
        xw = []
        for mt in range(MT):
            xw_t = work.tile([P, K], BF16, name="xw", tag="xw", bufs=4)
            if mt != 1:
                nc.scalar.copy(out=xw_t[:], in_=xb[mt][:].bitcast(FP8))
            else:
                nc.vector.tensor_copy(out=xw_t[:], in_=xb[mt][:].bitcast(FP8))
            xw.append(xw_t)
        keep_clock(4)
        for mt in range(MT):
            words = xw[mt][:].bitcast(F32)
            bank = psum.tile([P, G, 2, P], F32, name="xbank", tag="tr")
            for g in range(G):
                for u in range(2):
                    nc.tensor.transpose(bank[:, g, u, :], words[:, 256 * g + u : 256 * (g + 1) : 2], ident_f[:])
            keep_clock(2)
            for g in range(G):
                nc.vector.tensor_tensor(
                    out=xg[g][:, mt * P : (mt + 1) * P, :].rearrange("p r (u e) -> p r u e", u=2),
                    in0=bank[:, g, :, :].bitcast(BF16).rearrange("p u (r e) -> p r u e", e=2),
                    in1=x_sc[:, g, :].rearrange("p (u e) -> p u e", u=2).unsqueeze(1).to_broadcast([P, P, 2, 2]),
                    op=ALU.mult,
                )
        for g in range(G):
            nc.vector.quantize_mx(
                out=xc[g][:].bitcast(E4X4), scales=xs[g][:], in_=xg[g][:].rearrange("p r t -> p (r t)")
            )

        cst = keep.tile([P, P], F32, name="cst")
        cbank = psum.tile([P, P], BF16, name="cbank", tag="tr")
        nc.tensor.transpose(cbank[:], rows[:], ident_b[:])
        nc.scalar.copy(out=cst[:], in_=cbank[:])

        phi_t = keep.tile([P, DT, M], BF16, name="phi_t")

        def turn_phi(jd):
            pbank = psum.tile([P, MT, P], BF16, name="pbank", tag="tr")
            for mt in range(MT):
                nc.tensor.transpose(pbank[:, mt, :], phi_sb[:, mt, jd * P : (jd + 1) * P], ident_b[:])
            nc.scalar.copy(out=phi_t[:, jd, :], in_=pbank[:].rearrange("p t c -> p (t c)"))

        gam = [keep.tile([P, M], F32, name="gam%d" % jd) for jd in range(DT)]
        pc = {}
        ps = {}
        u_tiles = {}
        psi_tiles = {}
        y_tiles = {}
        grouped = {}

        def product(out, w, sc_ap, jd, s_lo):
            for g in range(G):
                nc.tensor.matmul_mx(
                    out=out,
                    lhsT=w[:, g, 2 * P * jd : 2 * P * (jd + 1)].bitcast(E2X4),
                    lhsT_scale=sc_ap[:, g, s_lo + P * jd : s_lo + P * (jd + 1)],
                    rhs=xc[g][:].bitcast(E4X4),
                    rhs_scale=xs[g][:],
                    start=(g == 0),
                    stop=(g == G - 1),
                )

        order = [(0, 0), (1, 0), (0, 1), (1, 1), (2, 0), (2, 1), (3, 0), (3, 1)]

        def discount(jd):
            acc = psum.tile([P, M], F32, name="acc", tag="mm")
            product(acc[:], gam_w, gam_sc, jd, 0)
            nc.scalar.activation(out=gam[jd][:], in_=acc[:], func=ACT.Sigmoid, bias=cst[:, 32 + jd : 33 + jd])

        def feed(s):
            z, g = order[s]
            accs = []
            for jj in range(4):
                jd = 4 * g + jj
                if s == 0:
                    discount(jd)
                if (s, jj) in ((1, 1), (1, 3), (2, 1), (2, 3)):
                    discount(2 * s + 2 + (jj + 1) // 2 - 1)
                acc = psum.tile([P, M], F32, name="acc", tag="mm")
                product(acc[:], psi_w[z], psi_sc1 if z else psi_sc0, jd, (z - 1) * D if z else 0)
                accs.append(acc)
                if jj % 2 == 1:
                    if s == 1:
                        turn_phi(4 + jj - 1)
                        turn_phi(4 + jj)
                    gate(s, jj // 2, accs[jj - 1 : jj + 1])
                    for turn in turns[s, jj // 2]:
                        turn[0](*turn[1:])

        def gate(s, pair, accs):
            z, g = order[s]
            u = w4([P, 2, M], F32, "u")
            u_tiles[s, pair] = u
            for ji in range(2):
                jd = 4 * g + 2 * pair + ji
                nc.vector.scalar_tensor_tensor(
                    out=u[:, ji, :], in0=accs[ji][:], scalar=cst[:, z * DT + jd : z * DT + jd + 1], in1=gam[jd][:],
                    op0=ALU.add, op1=ALU.mult,
                )
                if s > 0 and pair == 1 and ji == 0:
                    combine(s, 0)
            if s == 0 and pair == 0:
                combine(s, 0)

        def combine(s, pair, parts=1):
            psi = work.tile([P, 2, M], BF16, name="psi", tag="psi", bufs=5)
            jd = 4 * order[s][1] + 2 * pair
            u = u_tiles.pop((s, pair))
            for i in range(parts):
                lo, hi = 2 * i // parts, 2 * (i + 1) // parts
                nc.vector.scalar_tensor_tensor(
                    out=psi[:, lo:hi, :], in0=u[:, lo:hi, :], scalar=0.0, in1=phi_t[:, jd + lo : jd + hi, :],
                    op0=ALU.max, op1=ALU.add,
                )
            psi_tiles[s, pair] = psi

        def turn_1(s, pair, copies=(nc.scalar.copy,)):
            if pair == 0:
                y_tiles[s] = w4([P, MT, 2, P], F32, "y")
            y = y_tiles[s]
            psi = psi_tiles.pop((s, pair))
            w = 2 // len(copies)
            for i, copy in enumerate(copies):
                bank = psum.tile([P, MT, w, P], BF16, name="t1bank", tag="tr")
                for ji in range(w):
                    for mc in range(MT):
                        nc.tensor.transpose(bank[:, mc, ji, :], psi[:, i * w + ji, mc * P : (mc + 1) * P], ident_b[:])
                src = bank[:].rearrange("p c j d -> p (c j d)").bitcast(F32)
                lo = 64 * pair + 32 * w * i
                copy(
                    out=y[:, :, :, lo : lo + 32 * w],
                    in_=src.rearrange("p (c q u) -> p c u q", c=MT, u=2),
                )

        def turn_2(s):
            y = y_tiles.pop(s)
            grp = w4([P, M, 4], BF16, "grp")
            grouped[s] = grp
            for cp in range(2):
                bank = psum.tile([P, 2, 2, P], F32, name="t2bank", tag="tr")
                for ci in range(2):
                    for u in range(2):
                        nc.tensor.transpose(bank[:, ci, u, :], y[:, 2 * cp + ci, u, :], ident_f[:])
                dst = grp[:, 256 * cp : 256 * (cp + 1), :].rearrange("p r t -> p (r t)").bitcast(F32)
                copy = nc.vector.tensor_copy if s == steps - 1 and cp == 1 else nc.scalar.copy
                copy(
                    out=dst.rearrange("p (c r u) -> p c r u", c=2, u=2),
                    in_=bank[:].rearrange("p c u r -> p c r u"),
                )

        def stage_q(s):
            pc[order[s]] = keep.tile([P, M], U32, name="pc%d" % s, align_bytes=64)
            ps[order[s]] = keep.tile([P, M], U8, name="ps%d" % s, align_bytes=64)
            nc.vector.quantize_mx(
                out=pc[order[s]][:].bitcast(E4X4), scales=ps[order[s]][:], in_=grouped.pop(s)[:].rearrange("p r t -> p (r t)")
            )

        steps = Z * G
        vals = {}

        def value(jt, z, tag):
            a = psum.tile([P, M], F32, name="val", tag=tag)
            for g in range(G):
                nc.tensor.matmul_mx(
                    out=a[:],
                    lhsT=pref_w[:, g, 2 * P * jt : 2 * P * (jt + 1)].bitcast(E2X4),
                    lhsT_scale=pref_sc[:, g, P * jt : P * (jt + 1)],
                    rhs=pc[z, g][:].bitcast(E4X4),
                    rhs_scale=ps[z, g][:],
                    start=(g == 0),
                    stop=(g == G - 1),
                )
            vals[jt, z] = a

        best = [keep.tile([P, M], F32, name="best%d" % j) for j in range(TT)]
        den = keep.tile([P, TT, M], F32, name="den")
        num = [keep.tile([P, M], F32, name="num%d" % j) for j in range(TT)]
        out0 = out_0.rearrange("(c p) j -> p c j", p=P)
        out1 = out_1.rearrange("(c p) j -> p c j", p=P)
        e_tiles = {}
        ev_tiles = {}
        part = {}

        def save_first(jt):
            v0 = work.tile([P, M], F32, name="v0", tag="v0")
            nc.scalar.copy(out=v0[:], in_=vals[jt, 0][:])
            part[jt] = v0

        def larger(jt, z):
            if z < Z - 1:
                m = work.tile([P, M], F32, name="m%d" % z, tag="m%d" % z)
            else:
                m = best[jt]
            nc.vector.tensor_tensor(out=m[:], in0=part[jt][:], in1=vals[jt, z][:], op=ALU.max)
            part[jt] = m

        def weight(jt, z):
            if z % 2 == 0:
                e_tiles[jt, z // 2] = w4([P, 2, M], F32, "e")
            e = e_tiles[jt, z // 2][:, z % 2, :]
            nc.vector.tensor_tensor(out=e, in0=vals[jt, z][:], in1=best[jt][:], op=ALU.subtract)
            nc.scalar.activation(out=e, in_=e, func=ACT.Exp, scale=cst[:, 40 + jt : 41 + jt])

        def weigh(jt, z):
            if z % 2 == 0:
                ev_tiles[jt, z // 2] = w4([P, 2, M], F32, "ev")
            nc.vector.tensor_tensor(
                out=ev_tiles[jt, z // 2][:, z % 2, :], in0=e_tiles[jt, z // 2][:, z % 2, :],
                in1=vals[jt, z][:], op=ALU.mult,
            )

        def add_pairs(eng, tiles, jt):
            s = w4([P, 2, M], F32, "s")
            eng.tensor_tensor(out=s[:], in0=tiles[jt, 0][:], in1=tiles[jt, 1][:], op=ALU.add)
            return s

        def add_halves(eng, s, out):
            eng.tensor_tensor(out=out, in0=s[:, 0, :], in1=s[:, 1, :], op=ALU.add)

        def turn_out(src, tag):
            bank = psum.tile([P, MT, P], F32, name="obank", tag=tag)
            for mc in range(MT):
                nc.tensor.transpose(bank[:, mc, :], src[:, mc * P : (mc + 1) * P], ident_f[:])
            return bank

        def emit(bank, dram, jt, copy):
            ob = work.tile([P, MT, P], F32, name="ob", tag="ob", bufs=8)
            copy(out=ob[:], in_=bank[:])
            nc.sync.dma_start(out=dram[:, :, jt * P : (jt + 1) * P], in_=ob[:])

        for jd in range(4):
            turn_phi(jd)
            if jd == 1:
                keep_clock(2)
        turns = {(s, pair): [] for s in range(steps) for pair in range(2)}
        for s in range(2, steps):
            turns[s, 0] = [(turn_1, s - 2, 1)]
            turns[s, 1] = [(turn_2, s - 2), (turn_1, s - 1, 0)]
        turns[1, 1] = [(turn_1, 0, 0)]
        turns[7, 0] = [(turn_1, 5, 1), (turn_1, 6, 0)]
        turns[7, 1] = [(turn_2, 5), (turn_1, 6, 1)]
        for s in range(steps):
            feed(s)
            combine(s, 1, parts=2 if s == steps - 1 else 1)
            if s == 2:
                nc.scalar.activation(out=warm[:], in_=ident_f[:, 0:1], func=ACT.Exp)
            if s >= 2:
                stage_q(s - 2)
        for z in range(Z - 1):
            value(0, z, "mm")
            if z == 0:
                turn_2(6)
        save_first(0)
        turn_1(7, 0)
        stage_q(6)
        larger(0, 1)
        larger(0, 2)
        keep_clock(2)
        turn_1(7, 1, (nc.scalar.copy, nc.vector.tensor_copy))
        keep_clock(2)
        turn_2(7)
        stage_q(7)

        def add_to(total, tiles, jt, z):
            if z > 0:
                first = tiles[jt, 0][:, 0, :] if z == 1 else total
                nc.gpsimd.tensor_tensor(out=total, in0=first, in1=tiles[jt, z // 2][:, z % 2, :], op=ALU.add)

        def soft_out(jt, tag):
            soft = work.tile([P, M], F32, name="soft", tag="soft", bufs=4)
            nc.vector.tensor_tensor(out=soft[:], in0=num[jt][:], in1=den[:, jt, :], op=ALU.mult)
            return turn_out(soft, tag)

        value(0, 3, "mm")
        for z in range(Z):
            value(1, z, "tr")
        larger(0, 3)
        for z in range(Z):
            weight(0, z)
            add_to(den[:, 0, :], e_tiles, 0, z)
            if z == 1:
                save_first(1)
        for z in range(Z):
            weigh(0, z)
            add_to(num[0][:], ev_tiles, 0, z)
            if z < Z - 1:
                larger(1, z + 1)
        bank_0 = turn_out(best[0], "mm")
        for z in range(Z):
            value(2, z, "mm")
        for z in range(Z):
            weight(1, z)
            add_to(den[:, 1, :], e_tiles, 1, z)
            if z == 1:
                save_first(2)
        emit(bank_0, out0, 0, nc.scalar.copy)
        for z in range(Z):
            weigh(1, z)
            if z < 2:
                add_to(num[1][:], ev_tiles, 1, z)
            if z < Z - 1:
                larger(2, z + 1)
        bank_1 = turn_out(best[1], "tr")
        for z in range(Z):
            value(3, z, "tr")
        emit(bank_1, out0, 1, nc.scalar.copy)
        save_first(3)
        for z in range(Z):
            weight(2, z)
            add_to(den[:, 2, :], e_tiles, 2, z)
            if z < Z - 1:
                larger(3, z + 1)
        for z in range(Z):
            weight(3, z)
            add_to(den[:, 3, :], e_tiles, 3, z)
        for z in range(2, Z):
            add_to(num[1][:], ev_tiles, 1, z)
        for z in range(Z):
            weigh(2, z)
        bank_2 = turn_out(best[2], "mm")
        bank_3 = turn_out(best[3], "mm")
        for z in range(Z):
            weigh(3, z)
        for jt in (2, 3):
            s = add_pairs(nc.vector, ev_tiles, jt)
            add_halves(nc.vector, s, num[jt][:])
        for jt in range(TT):
            if jt == 3:
                emit(bank_2, out0, 2, nc.scalar.copy)
                emit(bank_3, out0, 3, nc.scalar.copy)
            nc.scalar.activation(out=den[:, jt, :], in_=den[:, jt, :], func=ACT.Ln)
        for jt in (0, 2, 3, 1):
            nc.scalar.activation(out=den[:, jt, :], in_=den[:, jt, :], func=ACT.Exp, scale=-1.0)
        softs = [soft_out(jt, "mm" if jt < 2 else "tr") for jt in (0, 2, 3, 1)]
        emit(softs[0], out1, 0, nc.scalar.copy)
        emit(softs[1], out1, 2, nc.vector.tensor_copy)
        emit(softs[2], out1, 3, nc.scalar.copy)
        emit(softs[3], out1, 1, nc.vector.tensor_copy)
